import numpy as np
import ml_dtypes

BF16 = ml_dtypes.bfloat16


def bf(x):
    return np.asarray(x, np.float32).astype(BF16)


def f32(x):
    return np.asarray(x, np.float32)


def f64(x):
    return np.asarray(x).astype(np.float64)


def striped(idx):
    return np.tile(idx.reshape(-1, 16).T, (8, 1))


S, K, M, N, E, Q = 512, 128, 512, 192, 2, 96


def setup_inputs():
    return {"base": bf(np.random.standard_normal((M, S))), "x": bf(np.random.standard_normal((K, N))), "w": bf(np.random.standard_normal((E, K, M)) / np.sqrt(K)), "b": f32(0.5 * np.random.standard_normal((M, 1))), "offs": striped(np.random.permutation(S)[:N])}


def reference(base, x, w, b, offs):
    idx = offs[:16].T.reshape(-1)
    z = f64(base).copy()
    for e in range(E):
        z[:, idx[e * Q : (e + 1) * Q]] += f64(w)[e].T @ f64(x)[:, e * Q : (e + 1) * Q]
    return np.maximum(z + f64(b), 0.0)

@@ -1,0 +1,80 @@
+import concourse.mybir as mybir
+from concourse.masks import make_identity
+
+P = 128
+TOKENS = 512
+FEATURES = 512
+ENTRIES = 192
+EXPERTS = 2
+PIECE = ENTRIES // EXPERTS
+PIECE_COLUMNS = PIECE // 16
+BLOCKS = FEATURES // P
+
+BF16 = mybir.dt.bfloat16
+F32 = mybir.dt.float32
+U16 = mybir.dt.uint16
+
+FLOPS = 2 * P * FEATURES * ENTRIES
+
+
+def tile_scatter_matmul_kernel(tc, base, x, w, b, offs, out):
+    nc = tc.nc
+    with (
+        tc.tile_pool(name="held", bufs=1) as held,
+        tc.psum_pool(name="banks", bufs=1) as banks,
+    ):
+        offsets = held.tile([P, ENTRIES // 16], U16, name="offsets")
+        nc.sync.dma_start(offsets[:], offs)
+
+        identity = held.tile([P, P], BF16, name="identity")
+        make_identity(nc, identity[:])
+
+        base_tiles = [held.tile([P, TOKENS], BF16, name=f"base{a}") for a in range(BLOCKS)]
+        for a in range(BLOCKS):
+            queue = nc.sync if a % 2 == 0 else nc.scalar
+            queue.dma_start(base_tiles[a][:], base[a * P : (a + 1) * P, :])
+
+        x_tile = held.tile([P, ENTRIES], BF16, name="x_tile")
+        nc.gpsimd.dma_start(x_tile[:], x)
+        w_tiles = [held.tile([P, FEATURES], BF16, name=f"w{e}") for e in range(EXPERTS)]
+        for e in range(EXPERTS):
+            queue = nc.sync if e % 2 == 0 else nc.scalar
+            queue.dma_start(w_tiles[e][:], w[e, :, :])
+
+        bias = held.tile([P, BLOCKS], F32, name="bias")
+        with nc.allow_non_contiguous_dma(reason="one float32 value to a partition and block"):
+            nc.gpsimd.dma_start(bias[:], b.rearrange("(a p) o -> p (a o)", p=P))
+
+        windows = [banks.tile([P, TOKENS], F32, name=f"window{a}") for a in range(BLOCKS)]
+        for a in range(BLOCKS):
+            nc.tensor.matmul(windows[a][:], identity[:], base_tiles[a][:], start=True, stop=False)
+
+        for a in range(BLOCKS):
+            for e in range(EXPERTS):
+                nc.tensor.matmul(
+                    windows[a][:].indirect(offsets[:, e * PIECE_COLUMNS : (e + 1) * PIECE_COLUMNS]),
+                    w_tiles[e][:, a * P : (a + 1) * P],
+                    x_tile[:, e * PIECE : (e + 1) * PIECE],
+                    start=False,
+                    stop=(e == EXPERTS - 1),
+                )
+
+        for a in range(BLOCKS):
+            result = held.tile([P, TOKENS], F32, name=f"result{a}")
+            if a % 2 == 0:
+                nc.vector.tensor_scalar(
+                    out=result[:],
+                    in0=windows[a][:],
+                    scalar1=bias[:, a : a + 1],
+                    scalar2=0.0,
+                    op0=mybir.AluOpType.add,
+                    op1=mybir.AluOpType.max,
+                )
+            else:
+                nc.scalar.activation(
+                    out=result[:],
+                    in_=windows[a][:],
+                    func=mybir.ActivationFunctionType.Relu,
+                    bias=bias[:, a : a + 1],
+                )
+            nc.sync.dma_start(out[a * P : (a + 1) * P, :], result[:])

@@ -35,7 +35,7 @@ def tile_scatter_matmul_kernel(tc, base, x, w, b, offs, out):
             queue.dma_start(base_tiles[a][:], base[a * P : (a + 1) * P, :])
 
         x_tile = held.tile([P, ENTRIES], BF16, name="x_tile")
-        nc.gpsimd.dma_start(x_tile[:], x)
+        nc.sync.dma_start(x_tile[:], x)
         w_tiles = [held.tile([P, FEATURES], BF16, name=f"w{e}") for e in range(EXPERTS)]
         for e in range(EXPERTS):
             queue = nc.sync if e % 2 == 0 else nc.scalar
@@ -43,7 +43,14 @@ def tile_scatter_matmul_kernel(tc, base, x, w, b, offs, out):
 
         bias = held.tile([P, BLOCKS], F32, name="bias")
         with nc.allow_non_contiguous_dma(reason="one float32 value to a partition and block"):
-            nc.gpsimd.dma_start(bias[:], b.rearrange("(a p) o -> p (a o)", p=P))
+            nc.scalar.dma_start(bias[:], b.rearrange("(a p) o -> p (a o)", p=P))
+
+        zeros = held.tile([P, 1], F32, name="zeros")
+        nc.vector.memset(zeros[:], 0.0)
+        table_warmer = held.tile([P, 1], F32, name="table_warmer")
+        nc.scalar.activation(
+            out=table_warmer[:], in_=zeros[:], func=mybir.ActivationFunctionType.Relu
+        )
 
         windows = [banks.tile([P, TOKENS], F32, name=f"window{a}") for a in range(BLOCKS)]
         for a in range(BLOCKS):
@@ -70,6 +77,7 @@ def tile_scatter_matmul_kernel(tc, base, x, w, b, offs, out):
                     op0=mybir.AluOpType.add,
                     op1=mybir.AluOpType.max,
                 )
+                nc.sync.dma_start(out[a * P : (a + 1) * P, :], result[:])
             else:
                 nc.scalar.activation(
                     out=result[:],
@@ -77,4 +85,4 @@ def tile_scatter_matmul_kernel(tc, base, x, w, b, offs, out):
                     func=mybir.ActivationFunctionType.Relu,
                     bias=bias[:, a : a + 1],
                 )
-            nc.sync.dma_start(out[a * P : (a + 1) * P, :], result[:])
+                nc.scalar.dma_start(out[a * P : (a + 1) * P, :], result[:])

@@ -9,6 +9,7 @@ EXPERTS = 2
 PIECE = ENTRIES // EXPERTS
 PIECE_COLUMNS = PIECE // 16
 BLOCKS = FEATURES // P
+WARMING_MATMULS = 3
 
 BF16 = mybir.dt.bfloat16
 F32 = mybir.dt.float32
@@ -45,12 +46,15 @@ def tile_scatter_matmul_kernel(tc, base, x, w, b, offs, out):
         with nc.allow_non_contiguous_dma(reason="one float32 value to a partition and block"):
             nc.scalar.dma_start(bias[:], b.rearrange("(a p) o -> p (a o)", p=P))
 
-        zeros = held.tile([P, 1], F32, name="zeros")
+        zeros = held.tile([P, TOKENS], BF16, name="zeros")
         nc.vector.memset(zeros[:], 0.0)
         table_warmer = held.tile([P, 1], F32, name="table_warmer")
         nc.scalar.activation(
-            out=table_warmer[:], in_=zeros[:], func=mybir.ActivationFunctionType.Relu
+            out=table_warmer[:], in_=zeros[:, 0:1], func=mybir.ActivationFunctionType.Relu
         )
+        idle_bank = banks.tile([P, TOKENS], F32, name="idle_bank")
+        for _ in range(WARMING_MATMULS):
+            nc.tensor.matmul(idle_bank[:], zeros[:, 0:P], zeros[:], start=True, stop=True)
 
         windows = [banks.tile([P, TOKENS], F32, name=f"window{a}") for a in range(BLOCKS)]
         for a in range(BLOCKS):

@@ -30,6 +30,11 @@ def tile_scatter_matmul_kernel(tc, base, x, w, b, offs, out):
         identity = held.tile([P, P], BF16, name="identity")
         make_identity(nc, identity[:])
 
+        bias_rows = held.tile([BLOCKS, P], F32, name="bias_rows")
+        nc.scalar.dma_start(bias_rows[:], b.rearrange("(a p) o -> a (p o)", p=P))
+        small_identity = held.tile([BLOCKS, BLOCKS], F32, name="small_identity")
+        make_identity(nc, small_identity[:])
+
         base_tiles = [held.tile([P, TOKENS], BF16, name=f"base{a}") for a in range(BLOCKS)]
         for a in range(BLOCKS):
             queue = nc.sync if a % 2 == 0 else nc.scalar
@@ -42,9 +47,6 @@ def tile_scatter_matmul_kernel(tc, base, x, w, b, offs, out):
             queue = nc.sync if e % 2 == 0 else nc.scalar
             queue.dma_start(w_tiles[e][:], w[e, :, :])
 
-        bias = held.tile([P, BLOCKS], F32, name="bias")
-        with nc.allow_non_contiguous_dma(reason="one float32 value to a partition and block"):
-            nc.scalar.dma_start(bias[:], b.rearrange("(a p) o -> p (a o)", p=P))
 
         zeros = held.tile([P, TOKENS], BF16, name="zeros")
         nc.vector.memset(zeros[:], 0.0)
@@ -55,6 +57,11 @@ def tile_scatter_matmul_kernel(tc, base, x, w, b, offs, out):
         idle_bank = banks.tile([P, TOKENS], F32, name="idle_bank")
         for _ in range(WARMING_MATMULS):
             nc.tensor.matmul(idle_bank[:], zeros[:, 0:P], zeros[:], start=True, stop=True)
+
+        bias_bank = banks.tile([P, BLOCKS], F32, name="bias_bank")
+        nc.tensor.matmul(bias_bank[:], bias_rows[:], small_identity[:], start=True, stop=True)
+        bias = held.tile([P, BLOCKS], F32, name="bias")
+        nc.vector.tensor_copy(bias[:], bias_bank[:])
 
         windows = [banks.tile([P, TOKENS], F32, name=f"window{a}") for a in range(BLOCKS)]
         for a in range(BLOCKS):

@@ -24,9 +24,6 @@ def tile_scatter_matmul_kernel(tc, base, x, w, b, offs, out):
         tc.tile_pool(name="held", bufs=1) as held,
         tc.psum_pool(name="banks", bufs=1) as banks,
     ):
-        offsets = held.tile([P, ENTRIES // 16], U16, name="offsets")
-        nc.sync.dma_start(offsets[:], offs)
-
         identity = held.tile([P, P], BF16, name="identity")
         make_identity(nc, identity[:])
 
@@ -37,16 +34,15 @@ def tile_scatter_matmul_kernel(tc, base, x, w, b, offs, out):
 
         base_tiles = [held.tile([P, TOKENS], BF16, name=f"base{a}") for a in range(BLOCKS)]
         for a in range(BLOCKS):
-            queue = nc.sync if a % 2 == 0 else nc.scalar
-            queue.dma_start(base_tiles[a][:], base[a * P : (a + 1) * P, :])
+            nc.sync.dma_start(base_tiles[a][:], base[a * P : (a + 1) * P, :])
 
         x_tile = held.tile([P, ENTRIES], BF16, name="x_tile")
         nc.sync.dma_start(x_tile[:], x)
+        offsets = held.tile([P, ENTRIES // 16], U16, name="offsets")
+        nc.sync.dma_start(offsets[:], offs)
         w_tiles = [held.tile([P, FEATURES], BF16, name=f"w{e}") for e in range(EXPERTS)]
         for e in range(EXPERTS):
-            queue = nc.sync if e % 2 == 0 else nc.scalar
-            queue.dma_start(w_tiles[e][:], w[e, :, :])
-
+            nc.sync.dma_start(w_tiles[e][:], w[e, :, :])
 
         zeros = held.tile([P, TOKENS], BF16, name="zeros")
         nc.vector.memset(zeros[:], 0.0)

@@ -75,21 +75,25 @@ def tile_scatter_matmul_kernel(tc, base, x, w, b, offs, out):
 
         for a in range(BLOCKS):
             result = held.tile([P, TOKENS], F32, name=f"result{a}")
-            if a % 2 == 0:
-                nc.vector.tensor_scalar(
-                    out=result[:],
-                    in0=windows[a][:],
-                    scalar1=bias[:, a : a + 1],
-                    scalar2=0.0,
-                    op0=mybir.AluOpType.add,
-                    op1=mybir.AluOpType.max,
-                )
-                nc.sync.dma_start(out[a * P : (a + 1) * P, :], result[:])
-            else:
-                nc.scalar.activation(
-                    out=result[:],
-                    in_=windows[a][:],
-                    func=mybir.ActivationFunctionType.Relu,
-                    bias=bias[:, a : a + 1],
-                )
-                nc.scalar.dma_start(out[a * P : (a + 1) * P, :], result[:])
+            pieces = 2 if a == 0 else 1
+            width = TOKENS // pieces
+            for h in range(pieces):
+                columns = slice(h * width, (h + 1) * width)
+                if a % 2 == 0:
+                    nc.vector.tensor_scalar(
+                        out=result[:, columns],
+                        in0=windows[a][:, columns],
+                        scalar1=bias[:, a : a + 1],
+                        scalar2=0.0,
+                        op0=mybir.AluOpType.add,
+                        op1=mybir.AluOpType.max,
+                    )
+                    nc.sync.dma_start(out[a * P : (a + 1) * P, columns], result[:, columns])
+                else:
+                    nc.scalar.activation(
+                        out=result[:, columns],
+                        in_=windows[a][:, columns],
+                        func=mybir.ActivationFunctionType.Relu,
+                        bias=bias[:, a : a + 1],
+                    )
+                    nc.scalar.dma_start(out[a * P : (a + 1) * P, columns], result[:, columns])

@@ -44,15 +44,16 @@ def tile_scatter_matmul_kernel(tc, base, x, w, b, offs, out):
         for e in range(EXPERTS):
             nc.sync.dma_start(w_tiles[e][:], w[e, :, :])
 
-        zeros = held.tile([P, TOKENS], BF16, name="zeros")
+        zeros = held.tile([P, P], BF16, name="zeros")
         nc.vector.memset(zeros[:], 0.0)
         table_warmer = held.tile([P, 1], F32, name="table_warmer")
         nc.scalar.activation(
             out=table_warmer[:], in_=zeros[:, 0:1], func=mybir.ActivationFunctionType.Relu
         )
-        idle_bank = banks.tile([P, TOKENS], F32, name="idle_bank")
+        idle_bank = banks.tile([P, TOKENS // P, P], F32, name="idle_bank")
+        zeros_repeated = zeros[:].unsqueeze(1).to_broadcast([P, TOKENS // P, P])
         for _ in range(WARMING_MATMULS):
-            nc.tensor.matmul(idle_bank[:], zeros[:, 0:P], zeros[:], start=True, stop=True)
+            nc.tensor.matmul(idle_bank[:], zeros[:], zeros_repeated, start=True, stop=True)
 
         bias_bank = banks.tile([P, BLOCKS], F32, name="bias_bank")
         nc.tensor.matmul(bias_bank[:], bias_rows[:], small_identity[:], start=True, stop=True)

@@ -40,9 +40,11 @@ def tile_scatter_matmul_kernel(tc, base, x, w, b, offs, out):
         nc.sync.dma_start(x_tile[:], x)
         offsets = held.tile([P, ENTRIES // 16], U16, name="offsets")
         nc.sync.dma_start(offsets[:], offs)
-        w_tiles = [held.tile([P, FEATURES], BF16, name=f"w{e}") for e in range(EXPERTS)]
-        for e in range(EXPERTS):
-            nc.sync.dma_start(w_tiles[e][:], w[e, :, :])
+        w_tiles = [held.tile([P, EXPERTS, 2 * P], BF16, name=f"w_blocks{s}") for s in range(BLOCKS // 2)]
+        for s in range(BLOCKS // 2):
+            nc.sync.dma_start(
+                w_tiles[s][:], w[:, :, 2 * s * P : 2 * (s + 1) * P].rearrange("e k m -> k e m")
+            )
 
         zeros = held.tile([P, P], BF16, name="zeros")
         nc.vector.memset(zeros[:], 0.0)
@@ -68,7 +70,7 @@ def tile_scatter_matmul_kernel(tc, base, x, w, b, offs, out):
             for e in range(EXPERTS):
                 nc.tensor.matmul(
                     windows[a][:].indirect(offsets[:, e * PIECE_COLUMNS : (e + 1) * PIECE_COLUMNS]),
-                    w_tiles[e][:, a * P : (a + 1) * P],
+                    w_tiles[a // 2][:, e, (a % 2) * P : (a % 2 + 1) * P],
                     x_tile[:, e * PIECE : (e + 1) * PIECE],
                     start=False,
                     stop=(e == EXPERTS - 1),

@@ -99,4 +99,4 @@ def tile_scatter_matmul_kernel(tc, base, x, w, b, offs, out):
                         func=mybir.ActivationFunctionType.Relu,
                         bias=bias[:, a : a + 1],
                     )
-                    nc.scalar.dma_start(out[a * P : (a + 1) * P, columns], result[:, columns])
+                    nc.sync.dma_start(out[a * P : (a + 1) * P, columns], result[:, columns])

@@ -8,7 +8,9 @@ ENTRIES = 192
 EXPERTS = 2
 PIECE = ENTRIES // EXPERTS
 PIECE_COLUMNS = PIECE // 16
-BLOCKS = FEATURES // P
+WINDOWS = FEATURES // P
+PAIRS = WINDOWS // 2
+FILL_WIDTH = 44
 WARMING_MATMULS = 3
 
 BF16 = mybir.dt.bfloat16
@@ -27,24 +29,20 @@ def tile_scatter_matmul_kernel(tc, base, x, w, b, offs, out):
         identity = held.tile([P, P], BF16, name="identity")
         make_identity(nc, identity[:])
 
-        bias_rows = held.tile([BLOCKS, P], F32, name="bias_rows")
-        nc.scalar.dma_start(bias_rows[:], b.rearrange("(a p) o -> a (p o)", p=P))
-        small_identity = held.tile([BLOCKS, BLOCKS], F32, name="small_identity")
-        make_identity(nc, small_identity[:])
+        bias = held.tile([P, WINDOWS], F32, name="bias")
+        nc.scalar.dma_start(bias[:], b.rearrange("(p a) o -> p (a o)", a=WINDOWS))
 
-        base_tiles = [held.tile([P, TOKENS], BF16, name=f"base{a}") for a in range(BLOCKS)]
-        for a in range(BLOCKS):
-            nc.sync.dma_start(base_tiles[a][:], base[a * P : (a + 1) * P, :])
-
+        base_by_partition = base.rearrange("(p a) t -> p a t", a=WINDOWS)
+        base_pairs = [held.tile([P, 2, TOKENS], BF16, name=f"base_pair{s}") for s in range(PAIRS)]
+        nc.sync.dma_start(base_pairs[0][:], base_by_partition[:, 0:2, :])
         x_tile = held.tile([P, ENTRIES], BF16, name="x_tile")
         nc.sync.dma_start(x_tile[:], x)
         offsets = held.tile([P, ENTRIES // 16], U16, name="offsets")
         nc.sync.dma_start(offsets[:], offs)
-        w_tiles = [held.tile([P, EXPERTS, 2 * P], BF16, name=f"w_blocks{s}") for s in range(BLOCKS // 2)]
-        for s in range(BLOCKS // 2):
-            nc.sync.dma_start(
-                w_tiles[s][:], w[:, :, 2 * s * P : 2 * (s + 1) * P].rearrange("e k m -> k e m")
-            )
+        w_tiles = [held.tile([P, FEATURES], BF16, name=f"w{e}") for e in range(EXPERTS)]
+        for e in range(EXPERTS):
+            nc.sync.dma_start(w_tiles[e][:], w[e])
+        nc.sync.dma_start(base_pairs[1][:], base_by_partition[:, 2:4, :])
 
         zeros = held.tile([P, P], BF16, name="zeros")
         nc.vector.memset(zeros[:], 0.0)
@@ -57,28 +55,42 @@ def tile_scatter_matmul_kernel(tc, base, x, w, b, offs, out):
         for _ in range(WARMING_MATMULS):
             nc.tensor.matmul(idle_bank[:], zeros[:], zeros_repeated, start=True, stop=True)
 
-        bias_bank = banks.tile([P, BLOCKS], F32, name="bias_bank")
-        nc.tensor.matmul(bias_bank[:], bias_rows[:], small_identity[:], start=True, stop=True)
-        bias = held.tile([P, BLOCKS], F32, name="bias")
-        nc.vector.tensor_copy(bias[:], bias_bank[:])
+        windows = [banks.tile([P, TOKENS], F32, name=f"window{a}") for a in range(WINDOWS)]
 
-        windows = [banks.tile([P, TOKENS], F32, name=f"window{a}") for a in range(BLOCKS)]
-        for a in range(BLOCKS):
-            nc.tensor.matmul(windows[a][:], identity[:], base_tiles[a][:], start=True, stop=False)
+        def fill(a, width):
+            for c in range(0, TOKENS, width):
+                columns = slice(c, min(c + width, TOKENS))
+                nc.tensor.matmul(
+                    windows[a][:, columns],
+                    identity[:],
+                    base_pairs[a // 2][:, a % 2, columns],
+                    start=(c == 0),
+                    stop=False,
+                )
 
-        for a in range(BLOCKS):
+        def add_products(a):
             for e in range(EXPERTS):
                 nc.tensor.matmul(
                     windows[a][:].indirect(offsets[:, e * PIECE_COLUMNS : (e + 1) * PIECE_COLUMNS]),
-                    w_tiles[a // 2][:, e, (a % 2) * P : (a % 2 + 1) * P],
+                    w_tiles[e][:, a::WINDOWS],
                     x_tile[:, e * PIECE : (e + 1) * PIECE],
                     start=False,
                     stop=(e == EXPERTS - 1),
                 )
 
-        for a in range(BLOCKS):
+        fill(0, TOKENS)
+        fill(1, TOKENS)
+        add_products(0)
+        add_products(1)
+        fill(2, FILL_WIDTH)
+        fill(3, FILL_WIDTH)
+        add_products(2)
+        add_products(3)
+
+        out_by_partition = out.rearrange("(p a) t -> p a t", a=WINDOWS)
+        for a in range(WINDOWS):
             result = held.tile([P, TOKENS], F32, name=f"result{a}")
-            pieces = 2 if a == 0 else 1
+            pieces = 1 if a == 1 else 2
             width = TOKENS // pieces
             for h in range(pieces):
                 columns = slice(h * width, (h + 1) * width)
@@ -91,7 +103,6 @@ def tile_scatter_matmul_kernel(tc, base, x, w, b, offs, out):
                         op0=mybir.AluOpType.add,
                         op1=mybir.AluOpType.max,
                     )
-                    nc.sync.dma_start(out[a * P : (a + 1) * P, columns], result[:, columns])
                 else:
                     nc.scalar.activation(
                         out=result[:, columns],
@@ -99,4 +110,4 @@ def tile_scatter_matmul_kernel(tc, base, x, w, b, offs, out):
                         func=mybir.ActivationFunctionType.Relu,
                         bias=bias[:, a : a + 1],
                     )
-                    nc.sync.dma_start(out[a * P : (a + 1) * P, columns], result[:, columns])
+                nc.sync.dma_start(out_by_partition[:, a, columns], result[:, columns])

@@ -8,8 +8,8 @@ ENTRIES = 192
 EXPERTS = 2
 PIECE = ENTRIES // EXPERTS
 PIECE_COLUMNS = PIECE // 16
-WINDOWS = FEATURES // P
-PAIRS = WINDOWS // 2
+PAIRS = FEATURES // (2 * P)
+WINDOWS = 2 * PAIRS
 FILL_WIDTH = 44
 WARMING_MATMULS = 3
 
@@ -29,20 +29,20 @@ def tile_scatter_matmul_kernel(tc, base, x, w, b, offs, out):
         identity = held.tile([P, P], BF16, name="identity")
         make_identity(nc, identity[:])
 
-        bias = held.tile([P, WINDOWS], F32, name="bias")
-        nc.scalar.dma_start(bias[:], b.rearrange("(p a) o -> p (a o)", a=WINDOWS))
+        bias = held.tile([P, PAIRS, 2], F32, name="bias")
+        nc.scalar.dma_start(bias[:], b.rearrange("(s p h) o -> p s (h o)", s=PAIRS, h=2))
 
-        base_by_partition = base.rearrange("(p a) t -> p a t", a=WINDOWS)
         base_pairs = [held.tile([P, 2, TOKENS], BF16, name=f"base_pair{s}") for s in range(PAIRS)]
-        nc.sync.dma_start(base_pairs[0][:], base_by_partition[:, 0:2, :])
+        w_pairs = [held.tile([P, EXPERTS, 2 * P], BF16, name=f"w_pair{s}") for s in range(PAIRS)]
         x_tile = held.tile([P, ENTRIES], BF16, name="x_tile")
-        nc.sync.dma_start(x_tile[:], x)
         offsets = held.tile([P, ENTRIES // 16], U16, name="offsets")
-        nc.sync.dma_start(offsets[:], offs)
-        w_tiles = [held.tile([P, FEATURES], BF16, name=f"w{e}") for e in range(EXPERTS)]
-        for e in range(EXPERTS):
-            nc.sync.dma_start(w_tiles[e][:], w[e])
-        nc.sync.dma_start(base_pairs[1][:], base_by_partition[:, 2:4, :])
+        for s in range(PAIRS):
+            features = slice(2 * P * s, 2 * P * (s + 1))
+            nc.sync.dma_start(base_pairs[s][:], base[features, :].rearrange("(p h) t -> p h t", h=2))
+            if s == 0:
+                nc.sync.dma_start(x_tile[:], x)
+                nc.sync.dma_start(offsets[:], offs)
+            nc.sync.dma_start(w_pairs[s][:], w[:, :, features].rearrange("e k m -> k e m"))
 
         zeros = held.tile([P, P], BF16, name="zeros")
         nc.vector.memset(zeros[:], 0.0)
@@ -72,7 +72,7 @@ def tile_scatter_matmul_kernel(tc, base, x, w, b, offs, out):
             for e in range(EXPERTS):
                 nc.tensor.matmul(
                     windows[a][:].indirect(offsets[:, e * PIECE_COLUMNS : (e + 1) * PIECE_COLUMNS]),
-                    w_tiles[e][:, a::WINDOWS],
+                    w_pairs[a // 2][:, e, a % 2 :: 2],
                     x_tile[:, e * PIECE : (e + 1) * PIECE],
                     start=False,
                     stop=(e == EXPERTS - 1),
@@ -87,7 +87,7 @@ def tile_scatter_matmul_kernel(tc, base, x, w, b, offs, out):
         add_products(2)
         add_products(3)
 
-        out_by_partition = out.rearrange("(p a) t -> p a t", a=WINDOWS)
+        out_by_partition = out.rearrange("(s p h) t -> p s h t", s=PAIRS, h=2)
         for a in range(WINDOWS):
             result = held.tile([P, TOKENS], F32, name=f"result{a}")
             pieces = 1 if a == 1 else 2
@@ -98,7 +98,7 @@ def tile_scatter_matmul_kernel(tc, base, x, w, b, offs, out):
                     nc.vector.tensor_scalar(
                         out=result[:, columns],
                         in0=windows[a][:, columns],
-                        scalar1=bias[:, a : a + 1],
+                        scalar1=bias[:, a // 2, a % 2 : a % 2 + 1],
                         scalar2=0.0,
                         op0=mybir.AluOpType.add,
                         op1=mybir.AluOpType.max,
@@ -108,6 +108,6 @@ def tile_scatter_matmul_kernel(tc, base, x, w, b, offs, out):
                         out=result[:, columns],
                         in_=windows[a][:, columns],
                         func=mybir.ActivationFunctionType.Relu,
-                        bias=bias[:, a : a + 1],
+                        bias=bias[:, a // 2, a % 2 : a % 2 + 1],
                     )
-                nc.sync.dma_start(out_by_partition[:, a, columns], result[:, columns])
+                nc.sync.dma_start(out_by_partition[:, a // 2, a % 2, columns], result[:, columns])

@@ -29,13 +29,11 @@ def tile_scatter_matmul_kernel(tc, base, x, w, b, offs, out):
         identity = held.tile([P, P], BF16, name="identity")
         make_identity(nc, identity[:])
 
-        bias = held.tile([P, PAIRS, 2], F32, name="bias")
-        nc.scalar.dma_start(bias[:], b.rearrange("(s p h) o -> p s (h o)", s=PAIRS, h=2))
-
         base_pairs = [held.tile([P, 2, TOKENS], BF16, name=f"base_pair{s}") for s in range(PAIRS)]
         w_pairs = [held.tile([P, EXPERTS, 2 * P], BF16, name=f"w_pair{s}") for s in range(PAIRS)]
         x_tile = held.tile([P, ENTRIES], BF16, name="x_tile")
         offsets = held.tile([P, ENTRIES // 16], U16, name="offsets")
+        bias = held.tile([P, PAIRS, 2], F32, name="bias")
         for s in range(PAIRS):
             features = slice(2 * P * s, 2 * P * (s + 1))
             nc.sync.dma_start(base_pairs[s][:], base[features, :].rearrange("(p h) t -> p h t", h=2))
@@ -43,6 +41,8 @@ def tile_scatter_matmul_kernel(tc, base, x, w, b, offs, out):
                 nc.sync.dma_start(x_tile[:], x)
                 nc.sync.dma_start(offsets[:], offs)
             nc.sync.dma_start(w_pairs[s][:], w[:, :, features].rearrange("e k m -> k e m"))
+            if s == 0:
+                nc.sync.dma_start(bias[:], b.rearrange("(s p h) o -> p s (h o)", s=PAIRS, h=2))
 
         zeros = held.tile([P, P], BF16, name="zeros")
         nc.vector.memset(zeros[:], 0.0)

@@ -90,7 +90,7 @@ def tile_scatter_matmul_kernel(tc, base, x, w, b, offs, out):
         out_by_partition = out.rearrange("(s p h) t -> p s h t", s=PAIRS, h=2)
         for a in range(WINDOWS):
             result = held.tile([P, TOKENS], F32, name=f"result{a}")
-            pieces = 1 if a == 1 else 2
+            pieces = 2 if a % 2 == 0 else 1
             width = TOKENS // pieces
             for h in range(pieces):
                 columns = slice(h * width, (h + 1) * width)

@@ -40,9 +40,11 @@ def tile_scatter_matmul_kernel(tc, base, x, w, b, offs, out):
             if s == 0:
                 nc.sync.dma_start(x_tile[:], x)
                 nc.sync.dma_start(offsets[:], offs)
-            nc.sync.dma_start(w_pairs[s][:], w[:, :, features].rearrange("e k m -> k e m"))
-            if s == 0:
+                for e in range(EXPERTS):
+                    nc.sync.dma_start(w_pairs[s][:, e, :], w[e, :, features])
                 nc.sync.dma_start(bias[:], b.rearrange("(s p h) o -> p s (h o)", s=PAIRS, h=2))
+            else:
+                nc.sync.dma_start(w_pairs[s][:], w[:, :, features].rearrange("e k m -> k e m"))
 
         zeros = held.tile([P, P], BF16, name="zeros")
         nc.vector.memset(zeros[:], 0.0)

import concourse.mybir as mybir
from concourse.masks import make_identity

P = 128
TOKENS = 512
FEATURES = 512
ENTRIES = 192
EXPERTS = 2
PIECE = ENTRIES // EXPERTS
PIECE_COLUMNS = PIECE // 16
PAIRS = FEATURES // (2 * P)
WINDOWS = 2 * PAIRS
FILL_WIDTH = 44
WARMING_MATMULS = 3

BF16 = mybir.dt.bfloat16
F32 = mybir.dt.float32
U16 = mybir.dt.uint16

FLOPS = 2 * P * FEATURES * ENTRIES


def tile_scatter_matmul_kernel(tc, base, x, w, b, offs, out):
    nc = tc.nc
    with (
        tc.tile_pool(name="held", bufs=1) as held,
        tc.psum_pool(name="banks", bufs=1) as banks,
    ):
        identity = held.tile([P, P], BF16, name="identity")
        make_identity(nc, identity[:])

        base_pairs = [held.tile([P, 2, TOKENS], BF16, name=f"base_pair{s}") for s in range(PAIRS)]
        w_pairs = [held.tile([P, EXPERTS, 2 * P], BF16, name=f"w_pair{s}") for s in range(PAIRS)]
        x_tile = held.tile([P, ENTRIES], BF16, name="x_tile")
        offsets = held.tile([P, ENTRIES // 16], U16, name="offsets")
        bias = held.tile([P, PAIRS, 2], F32, name="bias")
        for s in range(PAIRS):
            features = slice(2 * P * s, 2 * P * (s + 1))
            nc.sync.dma_start(base_pairs[s][:], base[features, :].rearrange("(p h) t -> p h t", h=2))
            if s == 0:
                nc.sync.dma_start(x_tile[:], x)
                nc.sync.dma_start(offsets[:], offs)
                for e in range(EXPERTS):
                    nc.sync.dma_start(w_pairs[s][:, e, :], w[e, :, features])
                nc.sync.dma_start(bias[:], b.rearrange("(s p h) o -> p s (h o)", s=PAIRS, h=2))
            else:
                nc.sync.dma_start(w_pairs[s][:], w[:, :, features].rearrange("e k m -> k e m"))

        zeros = held.tile([P, P], BF16, name="zeros")
        nc.vector.memset(zeros[:], 0.0)
        table_warmer = held.tile([P, 1], F32, name="table_warmer")
        nc.scalar.activation(
            out=table_warmer[:], in_=zeros[:, 0:1], func=mybir.ActivationFunctionType.Relu
        )
        idle_bank = banks.tile([P, TOKENS // P, P], F32, name="idle_bank")
        zeros_repeated = zeros[:].unsqueeze(1).to_broadcast([P, TOKENS // P, P])
        for _ in range(WARMING_MATMULS):
            nc.tensor.matmul(idle_bank[:], zeros[:], zeros_repeated, start=True, stop=True)

        windows = [banks.tile([P, TOKENS], F32, name=f"window{a}") for a in range(WINDOWS)]

        def fill(a, width):
            for c in range(0, TOKENS, width):
                columns = slice(c, min(c + width, TOKENS))
                nc.tensor.matmul(
                    windows[a][:, columns],
                    identity[:],
                    base_pairs[a // 2][:, a % 2, columns],
                    start=(c == 0),
                    stop=False,
                )

        def add_products(a):
            for e in range(EXPERTS):
                nc.tensor.matmul(
                    windows[a][:].indirect(offsets[:, e * PIECE_COLUMNS : (e + 1) * PIECE_COLUMNS]),
                    w_pairs[a // 2][:, e, a % 2 :: 2],
                    x_tile[:, e * PIECE : (e + 1) * PIECE],
                    start=False,
                    stop=(e == EXPERTS - 1),
                )

        fill(0, TOKENS)
        fill(1, TOKENS)
        add_products(0)
        add_products(1)
        fill(2, FILL_WIDTH)
        fill(3, FILL_WIDTH)
        add_products(2)
        add_products(3)

        out_by_partition = out.rearrange("(s p h) t -> p s h t", s=PAIRS, h=2)
        for a in range(WINDOWS):
            result = held.tile([P, TOKENS], F32, name=f"result{a}")
            pieces = 2 if a % 2 == 0 else 1
            width = TOKENS // pieces
            for h in range(pieces):
                columns = slice(h * width, (h + 1) * width)
                if a % 2 == 0:
                    nc.vector.tensor_scalar(
                        out=result[:, columns],
                        in0=windows[a][:, columns],
                        scalar1=bias[:, a // 2, a % 2 : a % 2 + 1],
                        scalar2=0.0,
                        op0=mybir.AluOpType.add,
                        op1=mybir.AluOpType.max,
                    )
                else:
                    nc.scalar.activation(
                        out=result[:, columns],
                        in_=windows[a][:, columns],
                        func=mybir.ActivationFunctionType.Relu,
                        bias=bias[:, a // 2, a % 2 : a % 2 + 1],
                    )
                nc.sync.dma_start(out_by_partition[:, a // 2, a % 2, columns], result[:, columns])
